import numpy as np
import ml_dtypes


def mxq(x, axis, fmt="e4m3"):
    dtype, down = {"e4m3": (ml_dtypes.float8_e4m3fn, 7), "e5m2": (ml_dtypes.float8_e5m2, 14)}[fmt]
    v = np.moveaxis(np.asarray(x, np.float32).astype(ml_dtypes.bfloat16).astype(np.float64), axis, -1)
    blocks = v.reshape(v.shape[:-1] + (-1, 32))
    amax = np.abs(blocks).max(-1, keepdims=True)
    byte = np.maximum(np.where(amax > 0, np.frexp(amax)[1] - 1 + 127, 0) - down, 1)
    scale = np.exp2(byte - 127.0)
    codes = (blocks / scale).astype(np.float32).astype(dtype).astype(np.float64)
    return np.moveaxis((codes * scale).reshape(v.shape), -1, axis)


WIDE = False


def mx_kscale(k, group=512):
    if not WIDE:
        return np.ones(k)
    levels = np.array([10, -10, 5, -5, 0])
    if group != 512:
        return np.exp2(np.random.permutation(np.resize(levels, k // group))).repeat(group)
    if k % 512:
        return np.exp2(np.random.permutation(np.resize(levels, k // 32))).repeat(32)
    a = np.empty((k // 512, 16))
    for p in range(k // 512):
        a[p, :8] = np.random.permutation(np.resize(levels, 8))
        for g in range(8):
            far = levels[np.abs(levels - a[p, g]) >= 10]
            a[p, g + 8] = far[np.random.randint(len(far))]
    return np.exp2(a.ravel()).repeat(32)


def f64(x):
    return np.asarray(x).astype(np.float64)


def striped(idx):
    return np.tile(np.asarray(idx).reshape(-1, 16).T, (8, 1)).astype(np.uint16)


def unstriped(offs):
    return offs[:16].T.reshape(-1).astype(np.int64)


H, KV, D, NQ, N = 8, 2, 128, 512, 512


def setup_inputs():
    n = np.random.standard_normal
    s = mx_kscale(D, 0)[:, None]
    u = mx_kscale(N)
    t = np.random.uniform(0.5, 2.0, N) * u
    v = n((KV, N, 128))
    v[:, :, 127] = 1.0
    return {
        "qT": (n((H, D, NQ)) * s * (0.70 / np.sqrt(D))).astype(np.float32),
        "kT": (n((KV, D, N)) / s).astype(np.float32),
        "t": t.reshape(N, 1).astype(np.float32),
        "v": (v / t[:, None]).astype(np.float32),
    }


def reference(qT, kT, t, v):
    a = np.repeat(mxq(f64(kT), 1, "e4m3"), H // KV, 0).transpose(0, 2, 1) @ mxq(f64(qT), 1, "e4m3")
    p = np.exp(a)
    w = p * f64(t)
    y = mxq(w, 1, "e4m3").transpose(0, 2, 1) @ np.repeat(mxq(f64(v), 1, "e4m3"), H // KV, 0)
    y = y / (y[:, :, 127:128])
    return y

@@ -1,0 +1,292 @@
+from contextlib import ExitStack
+
+import concourse.mybir as mybir
+
+H, KV, D, NQ, N = 8, 2, 128, 512, 512
+FLOPS = 2 * 2 * H * NQ * N * D
+
+F32 = mybir.dt.float32
+BF16 = mybir.dt.bfloat16
+I32 = mybir.dt.int32
+U32 = mybir.dt.uint32
+U8 = mybir.dt.uint8
+FP8X4 = mybir.dt.float8_e4m3fn_x4
+ACT = mybir.ActivationFunctionType
+ALU = mybir.AluOpType
+
+P = 128
+PACK = 4
+ROWS = 32
+TILES = 4
+QT = 128
+GROUPS = [(0, 1), (1, 2), (3, 2), (5, 2), (7, 1)]
+CHUNKS = [(0, 1), (1, 3), (4, 4)]
+PAIRS = [(0, 2), (1, 3)]
+
+
+def tile_rows_gqa_kernel(tc, qT, kT, t, v, out):
+    nc = tc.nc
+    with ExitStack() as ctx:
+        sb = ctx.enter_context(tc.tile_pool(name="sb", bufs=1))
+        ps = ctx.enter_context(tc.psum_pool(name="ps", bufs=1))
+        ctx.enter_context(tc.manual_schedule())
+
+        def head_of(g, qt):
+            return 4 * (g // 2) + 2 * (qt // 4) + g % 2
+
+        t_sb = sb.tile([P, PACK], F32, name="t_sb")
+        two = sb.tile([P, 1], F32, name="two")
+        ln2 = sb.tile([P, 1], F32, name="ln2")
+        warm = sb.tile([P, 1], F32, name="warm")
+        mant = sb.tile([P, PACK], I32, name="mant")
+        expo = sb.tile([P, PACK], I32, name="expo")
+        expo_ln = sb.tile([P, PACK], F32, name="expo_ln")
+        mant_ln = sb.tile([P, PACK], F32, name="mant_ln")
+        ln_t = sb.tile([P, PACK], F32, name="ln_t")
+        neg = sb.tile([P, PACK], F32, name="neg")
+        sign = sb.tile([P, PACK], F32, name="sign")
+        k_raw = [sb.tile([P, PACK, N // 2], F32, name="k_raw%d" % i) for i in range(2)]
+        k_bf = sb.tile([P, PACK, P, PACK], BF16, name="k_bf", align_bytes=64)
+        k_codes = sb.tile([P, N], U32, name="k_codes", align_bytes=64)
+        k_scales = sb.tile([P, N], U8, name="k_scales", align_bytes=64)
+        q_raw = [sb.tile([P, PACK, n * QT], F32, name="q_raw%d" % a) for a, n in CHUNKS]
+        q_bf = sb.tile([P, 8 * QT * PACK], BF16, name="q_bf", align_bytes=64)
+        q_codes = sb.tile([P, 8 * QT], U32, name="q_codes", align_bytes=64)
+        q_scales = sb.tile([P, 8 * QT], U8, name="q_scales", align_bytes=64)
+        v_raw = sb.tile([P, KV, PACK, D], F32, name="v_raw")
+        v_bf = sb.tile([P, KV * D * PACK], BF16, name="v_bf", align_bytes=64)
+        v_codes = sb.tile([P, KV * D], U32, name="v_codes", align_bytes=64)
+        v_scales = sb.tile([P, KV * D], U8, name="v_scales", align_bytes=64)
+        score = [ps.tile([P, 4 * QT], F32, name="score%d" % g) for g in range(TILES)]
+        y_ps = [ps.tile([P, 4, D], F32, name="y_ps%d" % i) for i in range(4)]
+        w_raw, w_bf, w_codes, w_scales = {}, {}, {}, {}
+        for g in range(TILES):
+            for i, (a, n) in enumerate(GROUPS):
+                w_raw[g, i] = sb.tile([P, PACK, n * QT], BF16, name="w_raw%d_%d" % (g, i))
+                w_bf[g, i] = sb.tile([P, n * QT * PACK], BF16, name="w_bf%d_%d" % (g, i), align_bytes=64)
+                w_codes[g, i] = sb.tile([P, n * QT], U32, name="w_codes%d_%d" % (g, i), align_bytes=64)
+                w_scales[g, i] = sb.tile([P, n * QT], U8, name="w_scales%d_%d" % (g, i), align_bytes=64)
+        recip, y_sb = {}, {}
+        for pr in range(2):
+            for i, (a, n) in enumerate(GROUPS):
+                recip[pr, i] = sb.tile([P, 2 * n], F32, name="recip%d_%d" % (pr, i))
+                y_sb[pr, i] = sb.tile([P, 2 * n, D], F32, name="y_sb%d_%d" % (pr, i))
+
+        def load_k(g, half):
+            eng = nc.sync if g < 2 else nc.scalar
+            src = kT[g // 2].rearrange("(p j) n -> p j n", j=PACK)
+            eng.dma_start(out=k_raw[half][ROWS * g : ROWS * (g + 1)], in_=src[:, :, 256 * half : 256 * (half + 1)])
+
+        def load_q(c, kv, eng):
+            a, n = CHUNKS[c]
+            h = head_of(2 * kv, a)
+            src = qT[h : h + 2].rearrange("h (p j) n -> (h p) j n", j=PACK)
+            q0 = (a % 4) * QT
+            eng.dma_start(out=q_raw[c][64 * kv : 64 * (kv + 1)], in_=src[:, :, q0 : q0 + n * QT])
+
+        def interleave(dst, src):
+            nc.vector.tensor_copy(
+                out=dst.rearrange("p (c i j) -> p c j i", i=4, j=PACK),
+                in_=src.rearrange("p j (c i) -> p c j i", i=4),
+            )
+
+        def quantize(codes, scales, src, w0, w1):
+            nc.vector.quantize_mx(
+                out=codes[:, w0:w1].bitcast(FP8X4), scales=scales[:, w0:w1], in_=src[:, PACK * w0 : PACK * w1]
+            )
+
+        def deal_k(half):
+            nc.vector.tensor_copy(
+                out=k_bf[:, :, 64 * half : 64 * (half + 1), :].rearrange("p r s j -> p s j r"),
+                in_=k_raw[half][:].rearrange("p j (s r) -> p s j r", r=PACK),
+            )
+
+        def quant_k(half):
+            quantize(k_codes, k_scales, k_bf[:].rearrange("p r s j -> p (r s j)"), 256 * half, 256 * (half + 1))
+
+        def inter_q(a, n):
+            c = max(i for i in range(len(CHUNKS)) if CHUNKS[i][0] <= a)
+            c0 = (a - CHUNKS[c][0]) * QT
+            interleave(q_bf[:, a * QT * PACK : (a + n) * QT * PACK], q_raw[c][:, :, c0 : c0 + n * QT])
+
+        def quant_q(a, n):
+            quantize(q_codes, q_scales, q_bf, a * QT, (a + n) * QT)
+
+        def inter_v(kv):
+            nc.vector.tensor_tensor(
+                out=v_bf[:, kv * D * PACK : (kv + 1) * D * PACK].rearrange("p (c i j) -> p c j i", i=4, j=PACK),
+                in0=v_raw[:, kv].rearrange("p j (c i) -> p c j i", i=4),
+                in1=sign[:].unsqueeze(1).unsqueeze(3).to_broadcast([P, D // 4, PACK, 4]),
+                op=ALU.mult,
+            )
+
+        def slots(i, f):
+            a, n = GROUPS[i]
+            per = 4 // n
+            return [(f * per + s // n, s % n) for s in range(4)]
+
+        def fill(pr, i, f):
+            a, n = GROUPS[i]
+            for s, (r, b) in enumerate(slots(i, f)):
+                for g in PAIRS[pr]:
+                    rows = slice(ROWS * g, ROWS * (g + 1))
+                    kc = slice(r * P, (r + 1) * P)
+                    qc = slice((a + b) * QT, (a + b + 1) * QT)
+                    nc.tensor.matmul_mx(
+                        out=score[g][:, s * QT : (s + 1) * QT],
+                        lhsT=k_codes[rows, kc].bitcast(FP8X4),
+                        lhsT_scale=k_scales[rows, kc],
+                        rhs=q_codes[rows, qc].bitcast(FP8X4),
+                        rhs_scale=q_scales[rows, qc],
+                        start=True,
+                        stop=True,
+                    )
+
+        def exps(pr, i, f):
+            a, n = GROUPS[i]
+            per = 4 // n
+            for g in PAIRS[pr]:
+                for x in range(per):
+                    r = f * per + x
+                    nc.scalar.activation(
+                        out=w_raw[g, i][:, r, :],
+                        in_=score[g][:, x * n * QT : (x + 1) * n * QT],
+                        func=ACT.Exp,
+                        bias=ln_t[:, r : r + 1],
+                    )
+
+        def weigh(pr, i):
+            n = GROUPS[i][1]
+            for g in PAIRS[pr]:
+                interleave(w_bf[g, i][:], w_raw[g, i][:])
+            for g in PAIRS[pr]:
+                quantize(w_codes[g, i], w_scales[g, i], w_bf[g, i], 0, n * QT)
+
+        def bank_of(pr, i):
+            return y_ps[(2 * i + pr) % 4]
+
+        def second(pr, i):
+            n = GROUPS[i][1]
+            for u, g in enumerate(PAIRS[pr]):
+                vc = slice((g // 2) * D, (g // 2 + 1) * D)
+                for b in range(n):
+                    wc = slice(b * QT, (b + 1) * QT)
+                    nc.tensor.matmul_mx(
+                        out=bank_of(pr, i)[:, u * n + b, :],
+                        lhsT=w_codes[g, i][:, wc].bitcast(FP8X4),
+                        lhsT_scale=w_scales[g, i][:, wc],
+                        rhs=v_codes[:, vc].bitcast(FP8X4),
+                        rhs_scale=v_scales[:, vc],
+                        start=True,
+                        stop=True,
+                    )
+
+        def invert(pr, i):
+            n = GROUPS[i][1]
+            nc.vector.reciprocal(out=recip[pr, i][:], in_=bank_of(pr, i)[:, : 2 * n, D - 1])
+
+        def divide_v(pr, i):
+            n = GROUPS[i][1]
+            nc.vector.tensor_tensor(
+                out=y_sb[pr, i][:],
+                in0=bank_of(pr, i)[:, : 2 * n, :],
+                in1=recip[pr, i][:].unsqueeze(2).to_broadcast([P, 2 * n, D]),
+                op=ALU.mult,
+            )
+
+        def divide_s(pr, i):
+            n = GROUPS[i][1]
+            for s in range(2 * n):
+                nc.scalar.activation(
+                    out=y_sb[pr, i][:, s, :], in_=bank_of(pr, i)[:, s, :], func=ACT.Copy, scale=recip[pr, i][:, s : s + 1]
+                )
+
+        def store(pr, i):
+            a, n = GROUPS[i]
+            for u, g in enumerate(PAIRS[pr]):
+                runs = [(0, n)] if (a // 4 == (a + n - 1) // 4) else [(b, 1) for b in range(n)]
+                for b, m in runs:
+                    q0 = ((a + b) % 4) * QT
+                    nc.sync.dma_start(
+                        out=out[head_of(g, a + b), q0 : q0 + m * QT, :].rearrange("(a p) e -> p a e", p=P),
+                        in_=y_sb[pr, i][:, u * n + b : u * n + b + m, :],
+                    )
+
+        nc.gpsimd.memset(two[:], 2.0)
+        nc.sync.dma_start(out=t_sb[:], in_=t.rearrange("(p j) o -> p (j o)", j=PACK))
+        load_k(0, 0)
+        load_k(2, 0)
+        load_k(1, 0)
+        load_k(3, 0)
+        load_k(0, 1)
+        load_k(2, 1)
+        load_k(1, 1)
+        nc.scalar.activation(out=ln2[:], in_=two[:], func=ACT.Ln)
+        load_k(3, 1)
+        load_q(0, 0, nc.sync)
+        load_q(0, 1, nc.scalar)
+        load_q(1, 0, nc.sync)
+        load_q(1, 1, nc.scalar)
+        nc.sync.dma_start(out=v_raw[:].rearrange("p kv j e -> p kv (j e)"), in_=v.rearrange("kv (p j) e -> p kv (j e)", j=PACK))
+        load_q(2, 0, nc.sync)
+        load_q(2, 1, nc.sync)
+
+        bits = t_sb[:].bitcast(I32)
+        nc.vector.tensor_scalar(out=mant[:], in0=bits, scalar1=0x007FFFFF, scalar2=0x3F800000, op0=ALU.bitwise_and, op1=ALU.bitwise_or)
+        nc.vector.tensor_scalar(out=expo[:], in0=bits, scalar1=23, scalar2=0xFF, op0=ALU.logical_shift_right, op1=ALU.bitwise_and)
+        nc.vector.tensor_scalar(out=neg[:], in0=t_sb[:], scalar1=0.0, scalar2=-2.0, op0=ALU.is_lt, op1=ALU.mult)
+        nc.vector.tensor_scalar(out=expo_ln[:], in0=expo[:], scalar1=-127.0, scalar2=ln2[:], op0=ALU.add, op1=ALU.mult)
+        nc.vector.tensor_scalar(out=sign[:], in0=neg[:], scalar1=1.0, scalar2=None, op0=ALU.add)
+        nc.scalar.activation(out=mant_ln[:], in_=mant[:].bitcast(F32), func=ACT.Ln)
+        nc.scalar.activation(out=warm[:], in_=two[:], func=ACT.Exp)
+        deal_k(0)
+        nc.vector.tensor_tensor(out=ln_t[:], in0=mant_ln[:], in1=expo_ln[:], op=ALU.add)
+        deal_k(1)
+        inter_q(0, 1)
+        quant_k(0)
+        quant_q(0, 1)
+        quant_k(1)
+
+        steps = [(pr, i, f) for i, (a, n) in enumerate(GROUPS) for f in range(n) for pr in range(2)]
+        G = [(pr, i) for i in range(len(GROUPS)) for pr in range(2)]
+        W = lambda k: (lambda: weigh(*G[k]))
+        I = lambda k: (lambda: invert(*G[k]))
+        DV = lambda k: (lambda: (divide_v(*G[k]), store(*G[k])))
+        DS = lambda k: (lambda: (divide_s(*G[k]), store(*G[k])))
+        IQ = lambda a, n: (lambda: inter_q(a, n))
+        QQ = lambda a, n: (lambda: quant_q(a, n))
+        IV = lambda kv: (lambda: inter_v(kv))
+        QV = lambda: quantize(v_codes, v_scales, v_bf, 0, KV * D)
+        vec = {
+            0: [IQ(1, 1), IQ(2, 2), QQ(1, 1), QQ(2, 2), W(0)],
+            1: [IV(0), IV(1), W(1)],
+            2: [QV, IQ(4, 2)],
+            3: [IQ(6, 2), QQ(4, 2)],
+            4: [QQ(6, 2), I(0), I(1), W(2)],
+            5: [DV(0), DV(1), W(3)],
+            7: [I(2)],
+            8: [W(4), I(3), DV(2)],
+            9: [DV(3), W(5)],
+            11: [I(4)],
+            12: [W(6), I(5), DV(4)],
+            13: [W(7)],
+            14: [I(6), W(8)],
+            15: [I(7), W(9)],
+            16: [I(8)],
+            17: [I(9), DV(9)],
+        }
+        pe = {4: [0, 1], 7: [2], 8: [3], 11: [4], 12: [5], 14: [6], 15: [7], 16: [8], 17: [9]}
+        act = {14: [DS(5)], 15: [DS(6)], 16: [DS(7)], 17: [DS(8)]}
+        last = len(steps)
+        fill(*steps[0])
+        for s in range(last + 2):
+            if s + 1 < last:
+                fill(*steps[s + 1])
+            for k in pe.get(s, []):
+                second(*G[k])
+            if s < last:
+                exps(*steps[s])
+            for job in act.get(s, []):
+                job()
+            for job in vec.get(s, []):
+                job()

@@ -58,7 +58,8 @@ def tile_rows_gqa_kernel(tc, qT, kT, t, v, out):
         v_codes = sb.tile([P, KV * D], U32, name="v_codes", align_bytes=64)
         v_scales = sb.tile([P, KV * D], U8, name="v_scales", align_bytes=64)
         score = [ps.tile([P, 4 * QT], F32, name="score%d" % g) for g in range(TILES)]
-        y_ps = [ps.tile([P, 4, D], F32, name="y_ps%d" % i) for i in range(4)]
+        y_ps = [ps.tile([P, 4, D], F32, name="y_ps%d" % i) for i in range(3)]
+        idle_ps = ps.tile([P, QT], F32, name="idle_ps")
         w_raw, w_bf, w_codes, w_scales = {}, {}, {}, {}
         for g in range(TILES):
             for i, (a, n) in enumerate(GROUPS):
@@ -95,11 +96,23 @@ def tile_rows_gqa_kernel(tc, qT, kT, t, v, out):
                 out=codes[:, w0:w1].bitcast(FP8X4), scales=scales[:, w0:w1], in_=src[:, PACK * w0 : PACK * w1]
             )
 
-        def deal_k(half):
+        def deal_k(half, r0, r1):
             nc.vector.tensor_copy(
-                out=k_bf[:, :, 64 * half : 64 * (half + 1), :].rearrange("p r s j -> p s j r"),
-                in_=k_raw[half][:].rearrange("p j (s r) -> p s j r", r=PACK),
+                out=k_bf[:, r0:r1, 64 * half : 64 * (half + 1), :].rearrange("p r s j -> p s j r"),
+                in_=k_raw[half][:].rearrange("p j (s r) -> p s j r", r=PACK)[:, :, :, r0:r1],
             )
+
+        def keep_warm(count):
+            for x in range(count):
+                nc.tensor.matmul_mx(
+                    out=idle_ps[:],
+                    lhsT=q_codes[:, :QT].bitcast(FP8X4),
+                    lhsT_scale=q_scales[:, :QT],
+                    rhs=q_codes[:, :QT].bitcast(FP8X4),
+                    rhs_scale=q_scales[:, :QT],
+                    start=True,
+                    stop=True,
+                )
 
         def quant_k(half):
             quantize(k_codes, k_scales, k_bf[:].rearrange("p r s j -> p (r s j)"), 256 * half, 256 * (half + 1))
@@ -163,7 +176,7 @@ def tile_rows_gqa_kernel(tc, qT, kT, t, v, out):
                 quantize(w_codes[g, i], w_scales[g, i], w_bf[g, i], 0, n * QT)
 
         def bank_of(pr, i):
-            return y_ps[(2 * i + pr) % 4]
+            return y_ps[(2 * i + pr) % 3]
 
         def second(pr, i):
             n = GROUPS[i][1]
@@ -214,17 +227,17 @@ def tile_rows_gqa_kernel(tc, qT, kT, t, v, out):
 
         nc.gpsimd.memset(two[:], 2.0)
         nc.sync.dma_start(out=t_sb[:], in_=t.rearrange("(p j) o -> p (j o)", j=PACK))
+        load_q(0, 0, nc.sync)
+        load_q(0, 1, nc.scalar)
         load_k(0, 0)
         load_k(2, 0)
         load_k(1, 0)
         load_k(3, 0)
         load_k(0, 1)
+        nc.scalar.activation(out=ln2[:], in_=two[:], func=ACT.Ln)
         load_k(2, 1)
         load_k(1, 1)
-        nc.scalar.activation(out=ln2[:], in_=two[:], func=ACT.Ln)
         load_k(3, 1)
-        load_q(0, 0, nc.sync)
-        load_q(0, 1, nc.scalar)
         load_q(1, 0, nc.sync)
         load_q(1, 1, nc.scalar)
         nc.sync.dma_start(out=v_raw[:].rearrange("p kv j e -> p kv (j e)"), in_=v.rearrange("kv (p j) e -> p kv (j e)", j=PACK))
@@ -239,12 +252,14 @@ def tile_rows_gqa_kernel(tc, qT, kT, t, v, out):
         nc.vector.tensor_scalar(out=sign[:], in0=neg[:], scalar1=1.0, scalar2=None, op0=ALU.add)
         nc.scalar.activation(out=mant_ln[:], in_=mant[:].bitcast(F32), func=ACT.Ln)
         nc.scalar.activation(out=warm[:], in_=two[:], func=ACT.Exp)
-        deal_k(0)
-        nc.vector.tensor_tensor(out=ln_t[:], in0=mant_ln[:], in1=expo_ln[:], op=ALU.add)
-        deal_k(1)
         inter_q(0, 1)
-        quant_k(0)
         quant_q(0, 1)
+        keep_warm(24)
+        deal_k(0, 0, 4)
+        nc.vector.tensor_tensor(out=ln_t[:], in0=mant_ln[:], in1=expo_ln[:], op=ALU.add)
+        deal_k(1, 0, 2)
+        deal_k(1, 2, 4)
+        quant_k(0)
         quant_k(1)
 
         steps = [(pr, i, f) for i, (a, n) in enumerate(GROUPS) for f in range(n) for pr in range(2)]
@@ -284,6 +299,8 @@ def tile_rows_gqa_kernel(tc, qT, kT, t, v, out):
                 fill(*steps[s + 1])
             for k in pe.get(s, []):
                 second(*G[k])
+            if s < last - 1:
+                keep_warm(5 - min(5, sum(2 * GROUPS[G[k][1]][1] for k in pe.get(s, []))))
             if s < last:
                 exps(*steps[s])
             for job in act.get(s, []):

from contextlib import ExitStack

import concourse.mybir as mybir

H, KV, D, NQ, N = 8, 2, 128, 512, 512
FLOPS = 2 * 2 * H * NQ * N * D

F32 = mybir.dt.float32
BF16 = mybir.dt.bfloat16
I32 = mybir.dt.int32
U32 = mybir.dt.uint32
U8 = mybir.dt.uint8
FP8X4 = mybir.dt.float8_e4m3fn_x4
ACT = mybir.ActivationFunctionType
ALU = mybir.AluOpType

P = 128
PACK = 4
ROWS = 32
TILES = 4
QT = 128
GROUPS = [(0, 1), (1, 2), (3, 2), (5, 2), (7, 1)]
CHUNKS = [(0, 1), (1, 3), (4, 4)]
PAIRS = [(0, 2), (1, 3)]


def tile_rows_gqa_kernel(tc, qT, kT, t, v, out):
    nc = tc.nc
    with ExitStack() as ctx:
        sb = ctx.enter_context(tc.tile_pool(name="sb", bufs=1))
        ps = ctx.enter_context(tc.psum_pool(name="ps", bufs=1))
        ctx.enter_context(tc.manual_schedule())

        def head_of(g, qt):
            return 4 * (g // 2) + 2 * (qt // 4) + g % 2

        t_sb = sb.tile([P, PACK], F32, name="t_sb")
        two = sb.tile([P, 1], F32, name="two")
        ln2 = sb.tile([P, 1], F32, name="ln2")
        warm = sb.tile([P, 1], F32, name="warm")
        mant = sb.tile([P, PACK], I32, name="mant")
        expo = sb.tile([P, PACK], I32, name="expo")
        expo_ln = sb.tile([P, PACK], F32, name="expo_ln")
        mant_ln = sb.tile([P, PACK], F32, name="mant_ln")
        ln_t = sb.tile([P, PACK], F32, name="ln_t")
        neg = sb.tile([P, PACK], F32, name="neg")
        sign = sb.tile([P, PACK], F32, name="sign")
        k_raw = [sb.tile([P, PACK, N // 2], F32, name="k_raw%d" % i) for i in range(2)]
        k_bf = sb.tile([P, PACK, P, PACK], BF16, name="k_bf", align_bytes=64)
        k_codes = sb.tile([P, N], U32, name="k_codes", align_bytes=64)
        k_scales = sb.tile([P, N], U8, name="k_scales", align_bytes=64)
        q_raw = [sb.tile([P, PACK, n * QT], F32, name="q_raw%d" % a) for a, n in CHUNKS]
        q_bf = sb.tile([P, 8 * QT * PACK], BF16, name="q_bf", align_bytes=64)
        q_codes = sb.tile([P, 8 * QT], U32, name="q_codes", align_bytes=64)
        q_scales = sb.tile([P, 8 * QT], U8, name="q_scales", align_bytes=64)
        v_raw = sb.tile([P, KV, PACK, D], F32, name="v_raw")
        v_bf = sb.tile([P, KV * D * PACK], BF16, name="v_bf", align_bytes=64)
        v_codes = sb.tile([P, KV * D], U32, name="v_codes", align_bytes=64)
        v_scales = sb.tile([P, KV * D], U8, name="v_scales", align_bytes=64)
        score = [ps.tile([P, 4 * QT], F32, name="score%d" % g) for g in range(TILES)]
        y_ps = [ps.tile([P, 4, D], F32, name="y_ps%d" % i) for i in range(3)]
        idle_ps = ps.tile([P, QT], F32, name="idle_ps")
        w_raw, w_bf, w_codes, w_scales = {}, {}, {}, {}
        for g in range(TILES):
            for i, (a, n) in enumerate(GROUPS):
                w_raw[g, i] = sb.tile([P, PACK, n * QT], BF16, name="w_raw%d_%d" % (g, i))
                w_bf[g, i] = sb.tile([P, n * QT * PACK], BF16, name="w_bf%d_%d" % (g, i), align_bytes=64)
                w_codes[g, i] = sb.tile([P, n * QT], U32, name="w_codes%d_%d" % (g, i), align_bytes=64)
                w_scales[g, i] = sb.tile([P, n * QT], U8, name="w_scales%d_%d" % (g, i), align_bytes=64)
        recip, y_sb = {}, {}
        for pr in range(2):
            for i, (a, n) in enumerate(GROUPS):
                recip[pr, i] = sb.tile([P, 2 * n], F32, name="recip%d_%d" % (pr, i))
                y_sb[pr, i] = sb.tile([P, 2 * n, D], F32, name="y_sb%d_%d" % (pr, i))

        def load_k(g, half):
            eng = nc.sync if g < 2 else nc.scalar
            src = kT[g // 2].rearrange("(p j) n -> p j n", j=PACK)
            eng.dma_start(out=k_raw[half][ROWS * g : ROWS * (g + 1)], in_=src[:, :, 256 * half : 256 * (half + 1)])

        def load_q(c, kv, eng):
            a, n = CHUNKS[c]
            h = head_of(2 * kv, a)
            src = qT[h : h + 2].rearrange("h (p j) n -> (h p) j n", j=PACK)
            q0 = (a % 4) * QT
            eng.dma_start(out=q_raw[c][64 * kv : 64 * (kv + 1)], in_=src[:, :, q0 : q0 + n * QT])

        def interleave(dst, src):
            nc.vector.tensor_copy(
                out=dst.rearrange("p (c i j) -> p c j i", i=4, j=PACK),
                in_=src.rearrange("p j (c i) -> p c j i", i=4),
            )

        def quantize(codes, scales, src, w0, w1):
            nc.vector.quantize_mx(
                out=codes[:, w0:w1].bitcast(FP8X4), scales=scales[:, w0:w1], in_=src[:, PACK * w0 : PACK * w1]
            )

        def deal_k(half, r0, r1):
            nc.vector.tensor_copy(
                out=k_bf[:, r0:r1, 64 * half : 64 * (half + 1), :].rearrange("p r s j -> p s j r"),
                in_=k_raw[half][:].rearrange("p j (s r) -> p s j r", r=PACK)[:, :, :, r0:r1],
            )

        def keep_warm(count):
            for x in range(count):
                nc.tensor.matmul_mx(
                    out=idle_ps[:],
                    lhsT=q_codes[:, :QT].bitcast(FP8X4),
                    lhsT_scale=q_scales[:, :QT],
                    rhs=q_codes[:, :QT].bitcast(FP8X4),
                    rhs_scale=q_scales[:, :QT],
                    start=True,
                    stop=True,
                )

        def quant_k(half):
            quantize(k_codes, k_scales, k_bf[:].rearrange("p r s j -> p (r s j)"), 256 * half, 256 * (half + 1))

        def inter_q(a, n):
            c = max(i for i in range(len(CHUNKS)) if CHUNKS[i][0] <= a)
            c0 = (a - CHUNKS[c][0]) * QT
            interleave(q_bf[:, a * QT * PACK : (a + n) * QT * PACK], q_raw[c][:, :, c0 : c0 + n * QT])

        def quant_q(a, n):
            quantize(q_codes, q_scales, q_bf, a * QT, (a + n) * QT)

        def inter_v(kv):
            nc.vector.tensor_tensor(
                out=v_bf[:, kv * D * PACK : (kv + 1) * D * PACK].rearrange("p (c i j) -> p c j i", i=4, j=PACK),
                in0=v_raw[:, kv].rearrange("p j (c i) -> p c j i", i=4),
                in1=sign[:].unsqueeze(1).unsqueeze(3).to_broadcast([P, D // 4, PACK, 4]),
                op=ALU.mult,
            )

        def slots(i, f):
            a, n = GROUPS[i]
            per = 4 // n
            return [(f * per + s // n, s % n) for s in range(4)]

        def fill(pr, i, f):
            a, n = GROUPS[i]
            for s, (r, b) in enumerate(slots(i, f)):
                for g in PAIRS[pr]:
                    rows = slice(ROWS * g, ROWS * (g + 1))
                    kc = slice(r * P, (r + 1) * P)
                    qc = slice((a + b) * QT, (a + b + 1) * QT)
                    nc.tensor.matmul_mx(
                        out=score[g][:, s * QT : (s + 1) * QT],
                        lhsT=k_codes[rows, kc].bitcast(FP8X4),
                        lhsT_scale=k_scales[rows, kc],
                        rhs=q_codes[rows, qc].bitcast(FP8X4),
                        rhs_scale=q_scales[rows, qc],
                        start=True,
                        stop=True,
                    )

        def exps(pr, i, f):
            a, n = GROUPS[i]
            per = 4 // n
            for g in PAIRS[pr]:
                for x in range(per):
                    r = f * per + x
                    nc.scalar.activation(
                        out=w_raw[g, i][:, r, :],
                        in_=score[g][:, x * n * QT : (x + 1) * n * QT],
                        func=ACT.Exp,
                        bias=ln_t[:, r : r + 1],
                    )

        def weigh(pr, i):
            n = GROUPS[i][1]
            for g in PAIRS[pr]:
                interleave(w_bf[g, i][:], w_raw[g, i][:])
            for g in PAIRS[pr]:
                quantize(w_codes[g, i], w_scales[g, i], w_bf[g, i], 0, n * QT)

        def bank_of(pr, i):
            return y_ps[(2 * i + pr) % 3]

        def second(pr, i):
            n = GROUPS[i][1]
            for u, g in enumerate(PAIRS[pr]):
                vc = slice((g // 2) * D, (g // 2 + 1) * D)
                for b in range(n):
                    wc = slice(b * QT, (b + 1) * QT)
                    nc.tensor.matmul_mx(
                        out=bank_of(pr, i)[:, u * n + b, :],
                        lhsT=w_codes[g, i][:, wc].bitcast(FP8X4),
                        lhsT_scale=w_scales[g, i][:, wc],
                        rhs=v_codes[:, vc].bitcast(FP8X4),
                        rhs_scale=v_scales[:, vc],
                        start=True,
                        stop=True,
                    )

        def invert(pr, i):
            n = GROUPS[i][1]
            nc.vector.reciprocal(out=recip[pr, i][:], in_=bank_of(pr, i)[:, : 2 * n, D - 1])

        def divide_v(pr, i):
            n = GROUPS[i][1]
            nc.vector.tensor_tensor(
                out=y_sb[pr, i][:],
                in0=bank_of(pr, i)[:, : 2 * n, :],
                in1=recip[pr, i][:].unsqueeze(2).to_broadcast([P, 2 * n, D]),
                op=ALU.mult,
            )

        def divide_s(pr, i):
            n = GROUPS[i][1]
            for s in range(2 * n):
                nc.scalar.activation(
                    out=y_sb[pr, i][:, s, :], in_=bank_of(pr, i)[:, s, :], func=ACT.Copy, scale=recip[pr, i][:, s : s + 1]
                )

        def store(pr, i):
            a, n = GROUPS[i]
            for u, g in enumerate(PAIRS[pr]):
                runs = [(0, n)] if (a // 4 == (a + n - 1) // 4) else [(b, 1) for b in range(n)]
                for b, m in runs:
                    q0 = ((a + b) % 4) * QT
                    nc.sync.dma_start(
                        out=out[head_of(g, a + b), q0 : q0 + m * QT, :].rearrange("(a p) e -> p a e", p=P),
                        in_=y_sb[pr, i][:, u * n + b : u * n + b + m, :],
                    )

        nc.gpsimd.memset(two[:], 2.0)
        nc.sync.dma_start(out=t_sb[:], in_=t.rearrange("(p j) o -> p (j o)", j=PACK))
        load_q(0, 0, nc.sync)
        load_q(0, 1, nc.scalar)
        load_k(0, 0)
        load_k(2, 0)
        load_k(1, 0)
        load_k(3, 0)
        load_k(0, 1)
        nc.scalar.activation(out=ln2[:], in_=two[:], func=ACT.Ln)
        load_k(2, 1)
        load_k(1, 1)
        load_k(3, 1)
        load_q(1, 0, nc.sync)
        load_q(1, 1, nc.scalar)
        nc.sync.dma_start(out=v_raw[:].rearrange("p kv j e -> p kv (j e)"), in_=v.rearrange("kv (p j) e -> p kv (j e)", j=PACK))
        load_q(2, 0, nc.sync)
        load_q(2, 1, nc.sync)

        bits = t_sb[:].bitcast(I32)
        nc.vector.tensor_scalar(out=mant[:], in0=bits, scalar1=0x007FFFFF, scalar2=0x3F800000, op0=ALU.bitwise_and, op1=ALU.bitwise_or)
        nc.vector.tensor_scalar(out=expo[:], in0=bits, scalar1=23, scalar2=0xFF, op0=ALU.logical_shift_right, op1=ALU.bitwise_and)
        nc.vector.tensor_scalar(out=neg[:], in0=t_sb[:], scalar1=0.0, scalar2=-2.0, op0=ALU.is_lt, op1=ALU.mult)
        nc.vector.tensor_scalar(out=expo_ln[:], in0=expo[:], scalar1=-127.0, scalar2=ln2[:], op0=ALU.add, op1=ALU.mult)
        nc.vector.tensor_scalar(out=sign[:], in0=neg[:], scalar1=1.0, scalar2=None, op0=ALU.add)
        nc.scalar.activation(out=mant_ln[:], in_=mant[:].bitcast(F32), func=ACT.Ln)
        nc.scalar.activation(out=warm[:], in_=two[:], func=ACT.Exp)
        inter_q(0, 1)
        quant_q(0, 1)
        keep_warm(24)
        deal_k(0, 0, 4)
        nc.vector.tensor_tensor(out=ln_t[:], in0=mant_ln[:], in1=expo_ln[:], op=ALU.add)
        deal_k(1, 0, 2)
        deal_k(1, 2, 4)
        quant_k(0)
        quant_k(1)

        steps = [(pr, i, f) for i, (a, n) in enumerate(GROUPS) for f in range(n) for pr in range(2)]
        G = [(pr, i) for i in range(len(GROUPS)) for pr in range(2)]
        W = lambda k: (lambda: weigh(*G[k]))
        I = lambda k: (lambda: invert(*G[k]))
        DV = lambda k: (lambda: (divide_v(*G[k]), store(*G[k])))
        DS = lambda k: (lambda: (divide_s(*G[k]), store(*G[k])))
        IQ = lambda a, n: (lambda: inter_q(a, n))
        QQ = lambda a, n: (lambda: quant_q(a, n))
        IV = lambda kv: (lambda: inter_v(kv))
        QV = lambda: quantize(v_codes, v_scales, v_bf, 0, KV * D)
        vec = {
            0: [IQ(1, 1), IQ(2, 2), QQ(1, 1), QQ(2, 2), W(0)],
            1: [IV(0), IV(1), W(1)],
            2: [QV, IQ(4, 2)],
            3: [IQ(6, 2), QQ(4, 2)],
            4: [QQ(6, 2), I(0), I(1), W(2)],
            5: [DV(0), DV(1), W(3)],
            7: [I(2)],
            8: [W(4), I(3), DV(2)],
            9: [DV(3), W(5)],
            11: [I(4)],
            12: [W(6), I(5), DV(4)],
            13: [W(7)],
            14: [I(6), W(8)],
            15: [I(7), W(9)],
            16: [I(8)],
            17: [I(9), DV(9)],
        }
        pe = {4: [0, 1], 7: [2], 8: [3], 11: [4], 12: [5], 14: [6], 15: [7], 16: [8], 17: [9]}
        act = {14: [DS(5)], 15: [DS(6)], 16: [DS(7)], 17: [DS(8)]}
        last = len(steps)
        fill(*steps[0])
        for s in range(last + 2):
            if s + 1 < last:
                fill(*steps[s + 1])
            for k in pe.get(s, []):
                second(*G[k])
            if s < last - 1:
                keep_warm(5 - min(5, sum(2 * GROUPS[G[k][1]][1] for k in pe.get(s, []))))
            if s < last:
                exps(*steps[s])
            for job in act.get(s, []):
                job()
            for job in vec.get(s, []):
                job()
